import numpy as np
import ml_dtypes


def mxq(x, axis, fmt="e4m3"):
    dtype, down = {"e4m3": (ml_dtypes.float8_e4m3fn, 7), "e5m2": (ml_dtypes.float8_e5m2, 14)}[fmt]
    v = np.moveaxis(np.asarray(x, np.float32).astype(ml_dtypes.bfloat16).astype(np.float64), axis, -1)
    blocks = v.reshape(v.shape[:-1] + (-1, 32))
    amax = np.abs(blocks).max(-1, keepdims=True)
    byte = np.maximum(np.where(amax > 0, np.frexp(amax)[1] - 1 + 127, 0) - down, 1)
    scale = np.exp2(byte - 127.0)
    codes = (blocks / scale).astype(np.float32).astype(dtype).astype(np.float64)
    return np.moveaxis((codes * scale).reshape(v.shape), -1, axis)


WIDE = False


def mx_kscale(k):
    if not WIDE:
        return np.ones(k)
    levels = np.array([10, -10, 5, -5, 0])
    if k % 512:
        return np.exp2(np.random.permutation(np.resize(levels, k // 32))).repeat(32)
    a = np.empty((k // 512, 16))
    for p in range(k // 512):
        a[p, :8] = np.random.permutation(np.resize(levels, 8))
        for g in range(8):
            far = levels[np.abs(levels - a[p, g]) >= 10]
            a[p, g + 8] = far[np.random.randint(len(far))]
    return np.exp2(a.ravel()).repeat(32)


BF16 = ml_dtypes.bfloat16


def bf(x):
    return np.asarray(x, np.float32).astype(BF16)


def f64(x):
    return np.asarray(x).astype(np.float64)


E2M1 = np.array([0.0, 0.5, 1.0, 1.5, 2.0, 3.0, 4.0, 6.0, -0.0, -0.5, -1.0, -1.5, -2.0, -3.0, -4.0, -6.0])


def pack_weight(w, fmt):
    k, n = w.shape
    w = f64(bf(w)).reshape(k // 32, 32, n)
    amax = np.abs(w).max(1)
    if fmt == "e4m3":
        byte = np.frexp(amax)[1] - 1 + 127 - 7
    else:
        mant, ex = np.frexp(amax / 6.0)
        byte = np.where(mant > 0.5, ex, ex - 1) + 127
    byte = np.clip(np.where(amax > 0, byte, 1), 1, 254)
    scaled = (w * np.exp2(127.0 - byte)[:, None, :]).reshape(k, n).astype(np.float32)
    by_word = np.ascontiguousarray(scaled.reshape(k // 512, 128, 4, n).transpose(0, 1, 3, 2))
    if fmt == "e4m3":
        words = by_word.astype(ml_dtypes.float8_e4m3fn).view(np.uint8)
    else:
        c = by_word.astype(ml_dtypes.float4_e2m1fn).view(np.uint8) & 0xF
        words = c[..., 0::2] | (c[..., 1::2] << 4)
    return np.ascontiguousarray(words), np.ascontiguousarray(byte.astype(np.uint8).reshape(k // 512, 16, n))


def unpack_weight(words, scales, fmt):
    g, p, n, _ = words.shape
    if fmt == "e4m3":
        vals = np.ascontiguousarray(words).view(ml_dtypes.float8_e4m3fn).astype(np.float64)
    else:
        nib = np.empty((g, p, n, 4), np.uint8)
        nib[..., 0::2] = words & 0xF
        nib[..., 1::2] = words >> 4
        vals = E2M1[nib]
    vals = vals * np.repeat(np.exp2(scales.astype(np.float64) - 127.0), 8, axis=1)[..., None]
    return vals.transpose(0, 1, 3, 2).reshape(g * 512, n)
def pack4(w):
    words, scales = pack_weight(w, "e2m1")
    return words.reshape(words.shape[0], 128, -1), scales


def unpack4(words, scales):
    return unpack_weight(words.reshape(words.shape[0], 128, -1, 2), scales, "e2m1")


M, K, B, C, G, N = 1024, 1024, 512, 4, 4, 1024
SPREAD = 0.4
SLOPE = 0.2


def setup_inputs():
    s, t = mx_kscale(K), mx_kscale(B)
    a = np.random.standard_normal((K, M)) * s[:, None]
    d = np.random.standard_normal((K, B * C)) * SPREAD / np.sqrt(K) / s[:, None]
    u = np.random.standard_normal((K, N)) / np.sqrt(K) / s[:, None]
    v = np.random.standard_normal((B, N)) / np.sqrt(B) / t[:, None]
    a_words, a_scales = pack4(a)
    d_words, d_scales = pack4(d)
    u_words, u_scales = pack4(u)
    v_words, v_scales = pack4(v)
    return {"a_words": a_words, "a_scales": a_scales,
            "d_words": d_words, "d_scales": d_scales,
            "u_words": u_words, "u_scales": u_scales,
            "v_words": v_words, "v_scales": v_scales,
            "gain": bf((1 + 0.1 * np.random.standard_normal(B)) * t),
            "bias": bf(0.3 * np.random.standard_normal(N)),
            "head": bf(np.random.standard_normal(N) / np.sqrt(N))}


def reference(a_words, a_scales, d_words, d_scales, u_words, u_scales, v_words, v_scales, gain, bias, head):
    x = unpack4(a_words, a_scales).T
    d = unpack4(d_words, d_scales)
    u = unpack4(u_words, u_scales)
    v = unpack4(v_words, v_scales)
    m = x @ d
    z = m.reshape(M // G, G, B, C)
    close = np.zeros((M // G, G, B))
    for r in range(1, G):
        close = close + np.exp(-np.abs(z - np.roll(z, r, axis=1)).sum(axis=-1))
    o = close.reshape(M, B) * f64(gain)
    pre = (x @ u) + (mxq(o, 1, "e4m3") @ v) + f64(bias)
    y = np.maximum(pre, SLOPE * pre)
    score = (y * f64(head)).sum(axis=1)
    return y, score

from contextlib import ExitStack

import concourse.mybir as mybir
from concourse.masks import make_identity

F32 = mybir.dt.float32
BF16 = mybir.dt.bfloat16
I32 = mybir.dt.int32
U32 = mybir.dt.uint32
U8 = mybir.dt.uint8
FP8X4 = mybir.dt.float8_e4m3fn_x4
FP4X4 = mybir.dt.float4_e2m1fn_x4
ACT = mybir.ActivationFunctionType
ALU = mybir.AluOpType
X = mybir.AxisListType.X

P = 128
M, K, B, C, G, N = 1024, 1024, 512, 4, 4, 1024
SLOPE = 0.2
FLOPS = 2 * M * K * B * C + 2 * M * K * N + 2 * M * B * N


def tile_minibatch_gan_discriminator_f2_kernel(
    tc, a_words, a_scales, d_words, d_scales, u_words, u_scales, v_words, v_scales, gain, bias, head, out_0, out_1
):
    nc = tc.nc
    with ExitStack() as ctx:
        keep = ctx.enter_context(tc.tile_pool(name="keep", bufs=1))
        work = ctx.enter_context(tc.tile_pool(name="work", bufs=3))
        psum = ctx.enter_context(tc.psum_pool(name="psum", bufs=2))

        ctx.enter_context(tc.manual_schedule())

        warm = keep.tile([P, 1], F32)
        ds_raw = keep.tile([P, 2, 2048], U8, align_bytes=64)
        as_pl = keep.tile([P, 2, 1024], U8, align_bytes=64)
        us_pl = keep.tile([P, 2, 1024], U8, align_bytes=64)
        vs_pl = keep.tile([P, 1024], U8, align_bytes=64)
        d_raw0 = keep.tile([P, 4096], U8, align_bytes=64)
        d_raw1 = keep.tile([P, 4096], U8, align_bytes=64)
        d_raw = [d_raw0, d_raw1]
        a_w = keep.tile([P, 2, 2048], U8, align_bytes=64)
        u_w = keep.tile([P, 2, 2048], U8, align_bytes=64)
        v_w = keep.tile([P, 2048], U8, align_bytes=64)
        d_w = []
        d_s = []
        for t in range(4):
            d_w.append(keep.tile([P, 2, 4, 256], U8, name=f"d_w{t}", align_bytes=64))
            d_s.append(keep.tile([P, 2, 4, 128], U8, name=f"d_s{t}", align_bytes=64))
        gain_b = keep.tile([P, 4], BF16)
        gain_f = keep.tile([P, 4], F32)
        rows_b = keep.tile([P, P], BF16)
        rows_f = keep.tile([P, P], F32)
        cols = keep.tile([P, 16], F32)
        bias02 = keep.tile([P, 8], F32)
        ident = keep.tile([P, P], F32)
        st = keep.tile([P, P], F32)
        score_row = keep.tile([P, P], F32)

        nc.vector.memset(warm[:], 0.0)
        nc.vector.memset(ds_raw[:].rearrange("p g n -> p (g n)").bitcast(I32), 0)
        nc.vector.memset(as_pl[:].rearrange("p g n -> p (g n)").bitcast(I32), 0)
        nc.scalar.activation(out=warm[:], in_=warm[:], func=ACT.Exp)

        def load_scales(plane, scales):
            rows = scales.rearrange("g (q r) n -> r q g n", r=4)
            for r in range(4):
                nc.sync.dma_start(out=plane[r:P:32].bitcast(I32), in_=rows[r].bitcast(I32))

        nc.sync.dma_start(out=d_raw[0][:].bitcast(I32), in_=d_words[0].bitcast(I32))
        load_scales(ds_raw[:], d_scales)
        nc.sync.dma_start(out=d_raw[1][:].bitcast(I32), in_=d_words[1].bitcast(I32))
        load_scales(as_pl[:], a_scales)
        for g in range(2):
            nc.sync.dma_start(out=a_w[:, g, :].bitcast(I32), in_=a_words[g].bitcast(I32))
        nc.sync.dma_start(out=gain_b[:], in_=gain.rearrange("(p t) -> p t", t=4))

        nc.gpsimd.memset(us_pl[:].rearrange("p g n -> p (g n)").bitcast(I32), 0)
        nc.gpsimd.memset(vs_pl[:].bitcast(I32), 0)
        nc.gpsimd.memset(rows_b[:], 0.0)
        nc.gpsimd.memset(st[:], 0.0)
        make_identity(nc, ident[:])
        load_scales(us_pl[:], u_scales)
        vrows = v_scales.rearrange("g (q r) n -> r q (g n)", r=4)
        for r in range(4):
            nc.sync.dma_start(out=vs_pl[r:P:32].bitcast(I32), in_=vrows[r].bitcast(I32))
        for g in range(2):
            nc.sync.dma_start(out=u_w[:, g, :].bitcast(I32), in_=u_words[g].bitcast(I32))
        nc.sync.dma_start(out=v_w[:].bitcast(I32), in_=v_words[0].bitcast(I32))
        nc.sync.dma_start(out=rows_b[0:8, :], in_=bias.rearrange("(c p) -> c p", p=P))
        nc.sync.dma_start(out=rows_b[8:16, :], in_=head.rearrange("(c p) -> c p", p=P))

        def permw(t, g):
            nc.vector.tensor_copy(
                out=d_w[t][:, g].rearrange("p c (q b) -> p c q b", b=2),
                in_=d_raw[g][:].rearrange("p (q j b) -> p j q b", j=16, b=2)[:, 4 * t : 4 * t + 4],
            )

        def perms(t, g):
            nc.vector.tensor_copy(
                out=d_s[t][:, g],
                in_=ds_raw[:, g, :].rearrange("p (q j) -> p j q", j=16)[:, 4 * t : 4 * t + 4],
            )

        CHAINS = [(0, 1), (2, 3), (4, 5), (6,), (7,)]
        VSUM = (4,)
        m_t = {}
        ms_t = {}
        dd_t = {}
        dist_t = {}
        ex_t = {}
        e_t = {}
        a_t = {}
        ob_t = {}
        oc_t = {}
        pre_t = {}
        ts_t = {}
        y_t = {}
        tr_t = {}
        ys_t = {}
        sp_t = {}
        xu_t = {}
        xx_t = {}

        def t1(q, t, j):
            blk = CHAINS[q][j]
            acc = psum.tile([P, 4, P], F32, name="m", bufs=3)
            m_t[q, t, j] = acc
            for c in range(4):
                for g in range(2):
                    nc.tensor.matmul_mx(
                        out=acc[:, c, :],
                        lhsT=d_w[t][:, g, c, :].bitcast(FP4X4),
                        lhsT_scale=d_s[t][:, g, c, :],
                        rhs=a_w[:, g, 256 * blk : 256 * blk + 256].bitcast(FP4X4),
                        rhs_scale=as_pl[:, g, 128 * blk : 128 * blk + 128],
                        start=(g == 0),
                        stop=(g == 1),
                    )

        def s1(q, t, j):
            if j == 0:
                ms_t[q, t] = work.tile([P, len(CHAINS[q]), 32, 3, 4], F32, name="ms", bufs=6)
            z = m_t[q, t, j][:].rearrange("p c (g s) -> p g s c", s=4)
            nc.scalar.copy(out=ms_t[q, t][:, j], in_=z[:, :, 1:4, :])

        def v1(q, t, j):
            if j == 0:
                dd_t[q, t] = work.tile([P, 2, 32 * len(CHAINS[q]), 3, 4], F32, name="dd", bufs=6)
            z = m_t[q, t, j][:].rearrange("p c (g s) -> p g s c", s=4)
            nc.vector.tensor_tensor(
                out=dd_t[q, t][:, 0, 32 * j : 32 * j + 32],
                in0=z[:, :, 0:1, :].to_broadcast([P, 32, 3, 4]),
                in1=ms_t[q, t][:, j],
                op=ALU.subtract,
            )

        def g1(q, t, part):
            mg = ms_t[q, t][:].rearrange("p j g s c -> p (j g) s c")
            dd = dd_t[q, t]
            if part == 0:
                nc.gpsimd.tensor_tensor(
                    out=dd[:, 1, :, 0:2, :],
                    in0=mg[:, :, 0:2, :],
                    in1=mg[:, :, 2:3, :].to_broadcast([P, 32 * len(CHAINS[q]), 2, 4]),
                    op=ALU.subtract,
                )
            else:
                nc.gpsimd.tensor_tensor(out=dd[:, 1, :, 2, :], in0=mg[:, :, 0, :], in1=mg[:, :, 1, :], op=ALU.subtract)

        def v2(q, t):
            dist_t[q, t] = work.tile([P, 192 * len(CHAINS[q])], F32, name="dist", bufs=6)
            nc.vector.tensor_reduce(
                out=dist_t[q, t][:],
                in_=dd_t[q, t][:].rearrange("p v g s c -> p (v g s) c"),
                axis=X,
                op=ALU.add,
                apply_absolute_value=True,
            )

        def s2(q, t, part):
            nb = len(CHAINS[q])
            if part == 0:
                ex_t[q, t] = work.tile([P, 192 * nb], F32, name="ex", bufs=3)
                nc.scalar.activation(out=ex_t[q, t][:], in_=dist_t[q, t][:], func=ACT.Exp, scale=-1.0)
            else:
                if t == 0:
                    e_t[q] = work.tile([P, 4, 2, 32 * nb, 3], F32, name="ee", bufs=4)
                nc.scalar.activation(
                    out=e_t[q][:, t].rearrange("p v g s -> p (v g s)"),
                    in_=ex_t[q, t][:],
                    func=ACT.Copy,
                    scale=gain_f[:, t : t + 1],
                )

        def g2(q, part):
            ng = 32 * len(CHAINS[q])
            eng = nc.vector if q in VSUM else nc.gpsimd
            e = e_t[q]
            near = e[:, :, 0]
            far = e[:, :, 1]
            if part == 0:
                a_t[q] = work.tile([P, 2, 4, ng, 2], F32, name="aa", bufs=2)
                eng.tensor_tensor(
                    out=a_t[q][:, 0],
                    in0=far[:, :, :, 2:3].to_broadcast([P, 4, ng, 2]),
                    in1=far[:, :, :, 0:2],
                    op=ALU.add,
                )
            aa = a_t[q]
            if part == 1:
                eng.tensor_tensor(
                    out=aa[:, 1],
                    in0=e[:, :, :, :, 0].rearrange("p t v g -> p t g v"),
                    in1=e[:, :, :, :, 1].rearrange("p t v g -> p t g v"),
                    op=ALU.add,
                )
            if part == 2:
                ob_t[q] = work.tile([P, ng, 4, 4], BF16, name="ob", bufs=2, align_bytes=64)
                eng.tensor_tensor(
                    out=ob_t[q][:, :, 1:3, :],
                    in0=aa[:, 0].rearrange("p t g s -> p g s t"),
                    in1=near[:, :, :, 0:2].rearrange("p t g s -> p g s t"),
                    op=ALU.add,
                )
            if part == 3:
                eng.tensor_tensor(
                    out=ob_t[q][:, :, 0:4:3, :],
                    in0=aa[:, 1].rearrange("p t g s -> p g s t"),
                    in1=near[:, :, :, 2:3].rearrange("p t g s -> p g s t").to_broadcast([P, ng, 2, 4]),
                    op=ALU.add,
                )

        def v3(q):
            nb = len(CHAINS[q])
            oc = work.tile([P, 128 * nb], U32, name="oc", bufs=3, align_bytes=64)
            osc = work.tile([P, 128 * nb], U8, name="osc", bufs=3, align_bytes=64)
            nc.vector.quantize_mx(
                out=oc[:].bitcast(FP8X4), scales=osc[:], in_=ob_t[q][:].rearrange("p g s t -> p (g s t)")
            )
            oc_t[q] = (oc, osc)

        def xu_pass(acc, ch, blk, g, last):
            nc.tensor.matmul_mx(
                out=acc,
                lhsT=u_w[:, g, 256 * ch : 256 * ch + 256].bitcast(FP4X4),
                lhsT_scale=us_pl[:, g, 128 * ch : 128 * ch + 128],
                rhs=a_w[:, g, 256 * blk : 256 * blk + 256].bitcast(FP4X4),
                rhs_scale=as_pl[:, g, 128 * blk : 128 * blk + 128],
                start=(g == 0),
                stop=last,
            )

        def ov_pass(acc, q, ch, j, first):
            oc, osc = oc_t[q]
            nc.tensor.matmul_mx(
                out=acc,
                lhsT=v_w[:, 256 * ch : 256 * ch + 256].bitcast(FP4X4),
                lhsT_scale=vs_pl[:, 128 * ch : 128 * ch + 128],
                rhs=oc[:, 128 * j : 128 * j + 128].bitcast(FP8X4),
                rhs_scale=osc[:, 128 * j : 128 * j + 128],
                start=first,
                stop=True,
            )

        def t2(q, cp):
            acc = psum.tile([P, 2, len(CHAINS[q]), P], F32, name="pre", bufs=2)
            pre_t[q, cp] = acc
            for h in range(2):
                ch = 2 * cp + h
                for j, blk in enumerate(CHAINS[q]):
                    for g in range(2):
                        xu_pass(acc[:, h, j, :], ch, blk, g, False)
                    ov_pass(acc[:, h, j, :], q, ch, j, False)

        def s3(q, cp, h):
            if h == 0:
                ts_t[q, cp] = work.tile([P, 2, 128 * len(CHAINS[q])], F32, name="ts", bufs=4)
            ch = 2 * cp + h
            nc.scalar.activation(
                out=ts_t[q, cp][:, h],
                in_=pre_t[q, cp][:, h].rearrange("p j n -> p (j n)"),
                func=ACT.Identity,
                scale=SLOPE,
                bias=bias02[:, ch : ch + 1],
            )

        def v4(q, cp, h):
            if cp == 0 and h == 0:
                y_t[q] = work.tile([P, 8, 128 * len(CHAINS[q])], F32, name="yt", bufs=3)
            ch = 2 * cp + h
            nc.vector.scalar_tensor_tensor(
                out=y_t[q][:, ch],
                in0=pre_t[q, cp][:, h].rearrange("p j n -> p (j n)"),
                scalar=cols[:, ch : ch + 1],
                in1=ts_t[q, cp][:, h],
                op0=ALU.add,
                op1=ALU.max,
            )

        def t2x(q, b):
            acc = psum.tile([P, 4, P], F32, name="pre", bufs=2)
            pre_t[q, "x", b] = acc
            for i in range(4):
                for g in range(2):
                    xu_pass(acc[:, i, :], 4 * b + i, CHAINS[q][0], g, g == 1)

        def sxu(q, b, i):
            if b == 0 and i == 0:
                xu_t[q] = work.tile([P, 8, P], F32, name="xu", bufs=1)
            ch = 4 * b + i
            nc.scalar.activation(
                out=xu_t[q][:, ch], in_=pre_t[q, "x", b][:, i, :], func=ACT.Identity, bias=cols[:, ch : ch + 1]
            )

        def t2o(q, b):
            acc = psum.tile([P, 4, P], F32, name="pre", bufs=2)
            pre_t[q, "o", b] = acc
            for i in range(4):
                ov_pass(acc[:, i, :], q, 4 * b + i, 0, True)

        def v4x(q, b):
            xx_t[q, b] = work.tile([P, 4, P], F32, name="xx", bufs=2)
            nc.vector.tensor_tensor(
                out=xx_t[q, b][:], in0=pre_t[q, "o", b][:], in1=xu_t[q][:, 4 * b : 4 * b + 4], op=ALU.add
            )

        def v4y(q, b):
            if b == 0:
                y_t[q] = work.tile([P, 8, P], F32, name="yt", bufs=3)
            xx = xx_t[q, b][:].rearrange("p i n -> p (i n)")
            nc.vector.scalar_tensor_tensor(
                out=y_t[q][:, 4 * b : 4 * b + 4].rearrange("p i n -> p (i n)"),
                in0=xx,
                scalar=SLOPE,
                in1=xx,
                op0=ALU.mult,
                op1=ALU.max,
            )

        def t3(q, j, half):
            tr = psum.tile([P, 4, P], F32, name="tr", bufs=2)
            tr_t[q, j, half] = tr
            for i in range(4):
                nc.tensor.transpose(tr[:, i, :], y_t[q][:, 4 * half + i, 128 * j : 128 * j + 128], ident[:])

        def s4(q, j, half):
            if half == 0:
                ys_t[q, j] = work.tile([P, N], F32, name="ys", bufs=3)
            nc.scalar.copy(
                out=ys_t[q, j][:, 512 * half : 512 * half + 512],
                in_=tr_t[q, j, half][:].rearrange("p i n -> p (i n)"),
            )

        def sty(q, j):
            blk = CHAINS[q][j]
            nc.sync.dma_start(out=out_0[128 * blk : 128 * blk + 128, :], in_=ys_t[q, j][:])

        def t3s(q, j):
            sp = psum.tile([P, 1], F32, name="sp", bufs=1)
            sp_t[q, j] = sp
            for ch in range(8):
                nc.tensor.matmul(
                    sp[:],
                    lhsT=y_t[q][:, ch, 128 * j : 128 * j + 128],
                    rhs=cols[:, 8 + ch : 9 + ch],
                    start=(ch == 0),
                    stop=(ch == 7),
                )

        def stc(q, j):
            blk = CHAINS[q][j]
            nc.vector.tensor_copy(out=st[:, blk : blk + 1], in_=sp_t[q, j][:])

        def columns():
            nc.vector.tensor_copy(out=rows_f[:], in_=rows_b[:])
            rp = psum.tile([P, 4, P], F32, name="tr", bufs=2)
            nc.tensor.transpose(rp[:, 0, :], rows_f[:], ident[:])
            nc.vector.tensor_copy(out=cols[:], in_=rp[:, 0, 0:16])
            nc.vector.tensor_scalar(out=bias02[:], in0=cols[:, 0:8], scalar1=SLOPE, scalar2=None, op0=ALU.mult)

        def gain_cast():
            nc.vector.tensor_copy(out=gain_f[:], in_=gain_b[:])

        permw(0, 0)
        permw(1, 0)
        perms(0, 0)
        perms(0, 1)
        permw(0, 1)
        permw(1, 1)
        perms(1, 0)
        t1(0, 0, 0)
        perms(1, 1)
        t1(0, 0, 1)
        permw(2, 0)
        s1(0, 0, 0)
        t1(0, 1, 0)
        permw(2, 1)
        s1(0, 0, 1)
        perms(2, 0)
        s1(0, 1, 0)
        v1(0, 0, 0)
        perms(2, 1)
        v1(0, 0, 1)
        t1(0, 1, 1)
        g1(0, 0, 0)
        v1(0, 1, 0)
        permw(3, 0)
        t1(0, 2, 0)
        s1(0, 1, 1)
        g1(0, 0, 1)
        t1(0, 2, 1)
        permw(3, 1)
        s1(0, 2, 0)
        g1(0, 1, 0)
        perms(3, 0)
        s1(0, 2, 1)
        perms(3, 1)
        v1(0, 1, 1)
        g1(0, 1, 1)
        v1(0, 2, 0)
        v2(0, 0)
        t1(0, 3, 0)
        g1(0, 2, 0)
        t1(0, 3, 1)
        s1(0, 3, 0)
        v1(0, 2, 1)
        s1(0, 3, 1)
        gain_cast()
        g1(0, 2, 1)
        v1(0, 3, 0)
        s2(0, 0, 0)
        v2(0, 1)
        t1(1, 0, 0)
        s2(0, 0, 1)
        g1(0, 3, 0)
        t1(1, 0, 1)
        s1(1, 0, 0)
        v1(0, 3, 1)
        s1(1, 0, 1)
        g1(0, 3, 1)
        v1(1, 0, 0)
        s2(0, 1, 0)
        columns()
        v2(0, 2)
        t1(1, 1, 0)
        s2(0, 1, 1)
        g1(1, 0, 0)
        t1(1, 1, 1)
        s1(1, 1, 0)
        v1(1, 0, 1)
        s1(1, 1, 1)
        g1(1, 0, 1)
        v1(1, 1, 0)
        s2(0, 2, 0)
        v2(0, 3)
        t1(1, 2, 0)
        s2(0, 2, 1)
        g1(1, 1, 0)
        t1(1, 2, 1)
        s1(1, 2, 0)
        v1(1, 1, 1)
        s1(1, 2, 1)
        g1(1, 1, 1)
        v1(1, 2, 0)
        s2(0, 3, 0)
        v2(1, 0)
        t1(1, 3, 0)
        s2(0, 3, 1)
        g1(1, 2, 0)
        t1(1, 3, 1)
        s1(1, 3, 0)
        v1(1, 2, 1)
        s1(1, 3, 1)
        g2(0, 0)
        v1(1, 3, 0)
        s2(1, 0, 0)
        v2(1, 1)
        t1(2, 0, 0)
        s2(1, 0, 1)
        g2(0, 1)
        t1(2, 0, 1)
        s1(2, 0, 0)
        v1(1, 3, 1)
        s1(2, 0, 1)
        g2(0, 2)
        v1(2, 0, 0)
        s2(1, 1, 0)
        t1(2, 1, 0)
        v1(2, 0, 1)
        s2(1, 1, 1)
        t1(2, 1, 1)
        g2(0, 3)
        s1(2, 1, 0)
        t1(2, 2, 0)
        s1(2, 1, 1)
        g1(1, 2, 1)
        v1(2, 1, 0)
        s1(2, 2, 0)
        v3(0)
        g1(1, 3, 0)
        v1(2, 1, 1)
        t1(2, 2, 1)
        v2(1, 2)
        t2(0, 0)
        g1(1, 3, 1)
        s1(2, 2, 1)
        t2(0, 1)
        g1(2, 0, 0)
        v1(2, 2, 0)
        s3(0, 0, 0)
        s3(0, 0, 1)
        t1(2, 3, 0)
        v2(1, 3)
        s2(1, 2, 0)
        g1(2, 0, 1)
        t1(2, 3, 1)
        s3(0, 1, 0)
        s3(0, 1, 1)
        g1(2, 1, 0)
        s2(1, 2, 1)
        v4(0, 0, 0)
        s1(2, 3, 0)
        v4(0, 0, 1)
        v4(0, 1, 0)
        s2(1, 3, 0)
        g1(2, 1, 1)
        v4(0, 1, 1)
        t2(0, 2)
        s1(2, 3, 1)
        v2(2, 0)
        s2(1, 3, 1)
        g1(2, 2, 0)
        t2(0, 3)
        s3(0, 2, 0)
        s3(0, 2, 1)
        v1(2, 2, 1)
        t3(0, 0, 0)
        g2(1, 0)
        v4(0, 2, 0)
        s2(2, 0, 0)
        v4(0, 2, 1)
        t1(3, 0, 0)
        s3(0, 3, 0)
        v1(2, 3, 0)
        s3(0, 3, 1)
        g2(1, 1)
        v2(2, 1)
        s2(2, 0, 1)
        t1(3, 1, 0)
        s1(3, 0, 0)
        s4(0, 0, 0)
        g2(1, 2)
        s1(3, 1, 0)
        v4(0, 3, 0)
        v4(0, 3, 1)
        s2(2, 1, 0)
        v1(2, 3, 1)
        g2(1, 3)
        v1(3, 0, 0)
        t3(0, 0, 1)
        s2(2, 1, 1)
        v1(3, 1, 0)
        t1(3, 2, 0)
        g1(2, 2, 1)
        s4(0, 0, 1)
        t1(3, 3, 0)
        v3(1)
        s1(3, 2, 0)
        g1(2, 3, 0)
        t3(0, 1, 0)
        sty(0, 0)
        v2(2, 2)
        s1(3, 3, 0)
        t3(0, 1, 1)
        s4(0, 1, 0)
        t2(1, 0)
        g1(2, 3, 1)
        s4(0, 1, 1)
        g1(3, 0, 0)
        t2(1, 1)
        v1(3, 2, 0)
        s3(1, 0, 0)
        v2(2, 3)
        g1(3, 0, 1)
        sty(0, 1)
        s3(1, 0, 1)
        t1(4, 0, 0)
        g1(3, 1, 0)
        s2(2, 2, 0)
        t1(4, 1, 0)
        s3(1, 1, 0)
        g1(3, 1, 1)
        s3(1, 1, 1)
        t3s(0, 0)
        v4(1, 0, 0)
        g1(3, 2, 0)
        s2(2, 2, 1)
        v4(1, 0, 1)
        s2(2, 3, 0)
        v4(1, 1, 0)
        g1(3, 2, 1)
        v4(1, 1, 1)
        s1(4, 0, 0)
        t2(1, 2)
        v1(3, 3, 0)
        s2(2, 3, 1)
        v2(3, 0)
        s1(4, 1, 0)
        t2(1, 3)
        g1(3, 3, 0)
        s3(1, 2, 0)
        v1(4, 0, 0)
        s3(1, 2, 1)
        t1(4, 2, 0)
        g2(2, 0)
        v2(3, 1)
        s2(3, 0, 0)
        s3(1, 3, 0)
        t3(1, 0, 0)
        s3(1, 3, 1)
        v4(1, 2, 0)
        t1(4, 3, 0)
        s2(3, 0, 1)
        v4(1, 2, 1)
        g2(2, 1)
        s1(4, 2, 0)
        v4(1, 3, 0)
        s2(3, 1, 0)
        v4(1, 3, 1)
        t2x(4, 0)
        s4(1, 0, 0)
        v1(4, 1, 0)
        g1(3, 3, 1)
        v2(3, 2)
        t2x(4, 1)
        s2(3, 1, 1)
        s1(4, 3, 0)
        g2(2, 2)
        t3(1, 0, 1)
        sxu(4, 0, 0)
        stc(0, 0)
        v1(4, 2, 0)
        sxu(4, 0, 1)
        t3(1, 1, 0)
        sxu(4, 0, 2)
        v2(3, 3)
        sxu(4, 0, 3)
        sxu(4, 1, 0)
        g2(2, 3)
        t3s(0, 1)
        sxu(4, 1, 1)
        sxu(4, 1, 2)
        sxu(4, 1, 3)
        v1(4, 3, 0)
        s2(3, 2, 0)
        s4(1, 0, 1)
        g1(4, 0, 0)
        s2(3, 2, 1)
        stc(0, 1)
        v3(2)
        s2(3, 3, 0)
        g1(4, 0, 1)
        sty(1, 0)
        t3(1, 1, 1)
        s4(1, 1, 0)
        g1(4, 1, 0)
        t2(2, 0)
        s2(3, 3, 1)
        v2(4, 0)
        s4(1, 1, 1)
        g1(4, 1, 1)
        t2(2, 1)
        g1(4, 2, 0)
        s3(2, 0, 0)
        v2(4, 1)
        sty(1, 1)
        g1(4, 2, 1)
        s3(2, 0, 1)
        t3s(1, 0)
        s2(4, 0, 0)
        g2(3, 0)
        v4(2, 0, 0)
        s3(2, 1, 0)
        v4(2, 0, 1)
        s3(2, 1, 1)
        g2(3, 1)
        v2(4, 2)
        s2(4, 0, 1)
        s2(4, 1, 0)
        t2(2, 2)
        g1(4, 3, 0)
        v4(2, 1, 0)
        s2(4, 1, 1)
        v4(2, 1, 1)
        g1(4, 3, 1)
        s2(4, 2, 0)
        stc(1, 0)
        g2(3, 2)
        s2(4, 2, 1)
        t2(2, 3)
        s3(2, 2, 0)
        v2(4, 3)
        g2(3, 3)
        s3(2, 2, 1)
        t3s(1, 1)
        v4(2, 2, 0)
        v4(2, 2, 1)
        s3(2, 3, 0)
        v3(3)
        s3(2, 3, 1)
        t3(2, 0, 0)
        s2(4, 3, 0)
        v4(2, 3, 0)
        t2(3, 0)
        stc(1, 1)
        s2(4, 3, 1)
        v4(2, 3, 1)
        s4(2, 0, 0)
        g2(4, 0)
        t2(3, 1)
        s3(3, 0, 0)
        g2(4, 1)
        s3(3, 0, 1)
        t3(2, 0, 1)
        g2(4, 2)
        v4(3, 0, 0)
        s3(3, 1, 0)
        t3s(2, 0)
        v4(3, 0, 1)
        s3(3, 1, 1)
        g2(4, 3)
        s4(2, 0, 1)
        v4(3, 1, 0)
        v4(3, 1, 1)
        v3(4)
        t2(3, 2)
        t2(3, 3)
        stc(2, 0)
        sty(2, 0)
        t3(3, 0, 0)
        s3(3, 2, 0)
        s3(3, 2, 1)
        s3(3, 3, 0)
        t3(2, 1, 0)
        s3(3, 3, 1)
        v4(3, 2, 0)
        v4(3, 2, 1)
        s4(3, 0, 0)
        t3s(2, 1)
        v4(3, 3, 0)
        v4(3, 3, 1)
        s4(2, 1, 0)
        t2o(4, 0)
        t2o(4, 1)
        stc(2, 1)
        t3(2, 1, 1)
        v4x(4, 0)
        t3(3, 0, 1)
        v4x(4, 1)
        s4(2, 1, 1)
        t3s(3, 0)
        v4y(4, 0)
        s4(3, 0, 1)
        v4y(4, 1)
        sty(2, 1)
        t3(4, 0, 0)
        stc(3, 0)
        t3(4, 0, 1)
        sty(3, 0)
        s4(4, 0, 0)
        t3s(4, 0)
        s4(4, 0, 1)
        stc(4, 0)
        sty(4, 0)

        tp = psum.tile([P, 4, P], F32, name="tr", bufs=2)
        nc.tensor.transpose(tp[:, 0, :], st[:], ident[:])
        nc.vector.tensor_copy(out=score_row[:], in_=tp[:, 0, :])
        nc.sync.dma_start(out=out_1.rearrange("(b p) -> b p", p=P), in_=score_row[0:8, :])
